import numpy as np
import ml_dtypes


def mxq(x, axis, fmt="e4m3"):
    dtype, down = {"e4m3": (ml_dtypes.float8_e4m3fn, 7), "e5m2": (ml_dtypes.float8_e5m2, 14)}[fmt]
    v = np.moveaxis(np.asarray(x, np.float32).astype(ml_dtypes.bfloat16).astype(np.float64), axis, -1)
    blocks = v.reshape(v.shape[:-1] + (-1, 32))
    amax = np.abs(blocks).max(-1, keepdims=True)
    byte = np.maximum(np.where(amax > 0, np.frexp(amax)[1] - 1 + 127, 0) - down, 1)
    scale = np.exp2(byte - 127.0)
    codes = (blocks / scale).astype(np.float32).astype(dtype).astype(np.float64)
    return np.moveaxis((codes * scale).reshape(v.shape), -1, axis)


WIDE = False


def mx_kscale(k):
    if not WIDE:
        return np.ones(k)
    levels = np.array([10, -10, 5, -5, 0])
    if k % 512:
        return np.exp2(np.random.permutation(np.resize(levels, k // 32))).repeat(32)
    a = np.empty((k // 512, 16))
    for p in range(k // 512):
        a[p, :8] = np.random.permutation(np.resize(levels, 8))
        for g in range(8):
            far = levels[np.abs(levels - a[p, g]) >= 10]
            a[p, g + 8] = far[np.random.randint(len(far))]
    return np.exp2(a.ravel()).repeat(32)


BF16 = ml_dtypes.bfloat16


def bf(x):
    return np.asarray(x, np.float32).astype(BF16)


def f64(x):
    return np.asarray(x).astype(np.float64)


M, S, R = 1024, 1536, 1024


def draw0():
    s = mx_kscale(S)
    u = mx_kscale(M)
    b = np.exp(2.0 * np.random.standard_normal((M, S)))
    b = b / b.mean(axis=1, keepdims=True)
    t = np.exp(1.5 * np.random.standard_normal((S, S)))
    t = t / t.sum(axis=1, keepdims=True)
    o = np.exp(np.random.standard_normal((M, S)))
    g = np.exp(2.0 * np.random.standard_normal((R, M)))
    g = g / g.sum(axis=1, keepdims=True)
    return {"beliefs": bf(b * s),
            "trans": bf(t / s[:, None]),
            "like": bf(o * u[:, None]),
            "mix": bf(g / u)}


def core(beliefs, trans, like, mix):
    pred = mxq(f64(beliefs), 1, "e4m3") @ mxq(f64(trans), 0, "e4m3")
    joint = pred * f64(like)
    pooled = mxq(f64(mix), 1, "e4m3") @ mxq(joint, 0, "e4m3")
    evidence = pooled.mean(axis=1, keepdims=True)
    return pooled / evidence


def e4m3fn_bytes(y):
    return np.clip(np.asarray(y, np.float64), -448.0, 448.0).astype(np.float32).astype(ml_dtypes.float8_e4m3fn).view(np.uint8)


def e4m3fn_values(b):
    return np.asarray(b, np.uint8).view(ml_dtypes.float8_e4m3fn).astype(np.float64)


def setup_inputs():
    d = draw0()
    x0 = np.asarray(d['trans']).astype(np.float64)
    s = (np.max(np.abs(x0), axis=(1,), keepdims=True) / 448.0).astype(np.float32)
    out = {}
    for k, v in d.items():
        if k == 'trans':
            out['trans_bytes'] = e4m3fn_bytes(x0 / s.astype(np.float64))
            out['trans_scale'] = s
        else:
            out[k] = v
    return out


def reference(beliefs, trans_bytes, trans_scale, like, mix):
    return core(beliefs, e4m3fn_values(trans_bytes) * trans_scale.astype(np.float64), like, mix)

@@ -1,0 +1,223 @@
+from contextlib import ExitStack
+
+import concourse.mybir as mybir
+from concourse.masks import make_identity
+
+M, S, R = 1024, 1536, 1024
+FLOPS = 2 * M * S * S + 2 * R * M * S + 3 * M * S
+
+F32 = mybir.dt.float32
+BF16 = mybir.dt.bfloat16
+U32 = mybir.dt.uint32
+U8 = mybir.dt.uint8
+F8 = mybir.dt.float8_e4m3fn
+X4 = mybir.dt.float8_e4m3fn_x4
+ALU = mybir.AluOpType
+ACT = mybir.ActivationFunctionType
+AX = mybir.AxisListType
+
+P = 128
+KP = 512
+JS = S // KP
+GS = M // KP
+NU = 128
+CW = 256
+LOADS = ((0, 512), (512, 512), (1024, 512))
+WIDEN_ON_VECTOR = (10, 0, 2, 4, 0, 5)
+INTERLEAVE_ON_SCALAR = (1, 1, 2, 1, 2, 2)
+
+
+def tile_pooled_belief_update_s7_kernel(tc, beliefs, trans_bytes, trans_scale, like, mix, out):
+    nc = tc.nc
+    with ExitStack() as ctx:
+        keep = ctx.enter_context(tc.tile_pool(name="keep", bufs=1))
+        stage = ctx.enter_context(tc.tile_pool(name="stage", bufs=4))
+        psum = ctx.enter_context(tc.psum_pool(name="psum", bufs=1))
+
+        ident = keep.tile([P, P], F32, name="ident")
+        make_identity(nc, ident[:])
+
+        t_view = trans_bytes.rearrange("(j p t) n -> j p t n", p=P, t=4)
+        b_view = beliefs.rearrange("(g p t) k -> g p t k", p=P, t=4)
+        l_view = like.rearrange("(g p t) n -> g p t n", p=P, t=4)
+        m_view = mix.rearrange("(p i) m -> p i m", i=8)
+        o_view = out.rearrange("(p i) n -> i p n", i=8)
+
+        tscale = keep.tile([P, JS, 4], F32, name="tscale")
+        nc.sync.dma_start(out=tscale[:], in_=trans_scale.rearrange("(j p t) o -> p j (t o)", p=P, t=4))
+
+        tb = {}
+        lk = {}
+        braw = {}
+        mraw = {}
+
+        def load_t(c):
+            c0, w = LOADS[c]
+            for j in range(JS):
+                tile = keep.tile([P, 4, w], U8, name=f"tb_{c}_{j}")
+                nc.sync.dma_start(out=tile[:], in_=t_view[j][:, :, c0 : c0 + w])
+                tb[c, j] = tile
+
+        def load_b(g):
+            for h in range(2):
+                tile = keep.tile([P, 2, S], BF16, name=f"braw_{g}_{h}")
+                nc.sync.dma_start(out=tile[:], in_=b_view[g][:, 2 * h : 2 * h + 2, :])
+                braw[g, h] = tile
+
+        def load_l(g, c):
+            c0, w = LOADS[c]
+            tile = keep.tile([P, 4, w], BF16, name=f"lk_{g}_{c}")
+            nc.sync.dma_start(out=tile[:], in_=l_view[g][:, :, c0 : c0 + w])
+            lk[g, c] = tile
+
+        def load_m(q):
+            tile = keep.tile([P, 2, M], BF16, name=f"mraw_{q}")
+            nc.sync.dma_start(out=tile[:], in_=m_view[:, 2 * q : 2 * q + 2, :])
+            mraw[q] = tile
+
+        load_t(0)
+        load_b(0)
+        load_b(1)
+        load_l(0, 0)
+        load_t(1)
+        load_l(1, 0)
+        load_t(2)
+        load_l(0, 1)
+        load_l(1, 1)
+        load_m(0)
+        load_l(0, 2)
+        load_l(1, 2)
+        load_m(1)
+        load_m(2)
+        load_m(3)
+
+        tq = [keep.tile([P, S], U32, name=f"tq_{j}", align_bytes=64) for j in range(JS)]
+        ts = [keep.tile([P, S], U8, name=f"ts_{j}", align_bytes=64) for j in range(JS)]
+        bq = [keep.tile([P, M], U32, name=f"bq_{j}", align_bytes=64) for j in range(JS)]
+        bs = [keep.tile([P, M], U8, name=f"bs_{j}", align_bytes=64) for j in range(JS)]
+        mq = [keep.tile([P, R], U32, name=f"mq_{g}", align_bytes=64) for g in range(GS)]
+        ms = [keep.tile([P, R], U8, name=f"ms_{g}", align_bytes=64) for g in range(GS)]
+        jq = [keep.tile([P, S], U32, name=f"jq_{g}", align_bytes=64) for g in range(GS)]
+        js = [keep.tile([P, S], U8, name=f"js_{g}", align_bytes=64) for g in range(GS)]
+
+        def quantize(codes, scales, c0, w, src):
+            nc.vector.quantize_mx(
+                out=codes[:, c0 : c0 + w].bitcast(X4), scales=scales[:, c0 : c0 + w], in_=src
+            )
+
+        def trans_chunk(q):
+            c0, w = q * CW, CW
+            for j in range(JS):
+                c = c0 // 512
+                off = c0 - 512 * c
+                wide = stage.tile([P, 4, w], BF16, name="wide", bufs=6)
+                for t in range(4):
+                    src = tb[c, j][:, t, off : off + w].bitcast(F8)
+                    if 4 * j + t < WIDEN_ON_VECTOR[q]:
+                        nc.vector.tensor_scalar(
+                            out=wide[:, t, :], in0=src, scalar1=tscale[:, j, t : t + 1], scalar2=None, op0=ALU.mult
+                        )
+                    else:
+                        nc.scalar.activation(
+                            out=wide[:, t, :], in_=src, func=ACT.Copy, scale=tscale[:, j, t : t + 1]
+                        )
+                grouped = stage.tile([P, w, 4], BF16, name="tgroup", bufs=6, align_bytes=64)
+                if JS - j <= INTERLEAVE_ON_SCALAR[q]:
+                    nc.scalar.copy(out=grouped[:], in_=wide[:].rearrange("p t n -> p n t"))
+                else:
+                    nc.vector.tensor_copy(out=grouped[:], in_=wide[:].rearrange("p t n -> p n t"))
+                quantize(tq[j], ts[j], c0, w, grouped[:].rearrange("p n t -> p (n t)"))
+
+        def turn(raw, pass_index, codes, scales, col0, on_scalar):
+            words = raw[:].rearrange("p a k -> p (a k)").bitcast(F32)
+            row_words = raw.shape[2] // 2
+            bank = psum.tile([P, 2, 2, P], F32, name="xt", bufs=3)
+            for a in range(2):
+                for u in range(2):
+                    w0 = a * row_words + 256 * pass_index
+                    nc.tensor.transpose(bank[:, a, u, :], words[:, w0 + u : w0 + 256 : 2], ident[:])
+            grouped = stage.tile([P, 2, P, 4], BF16, name="bgroup", bufs=4, align_bytes=64)
+            dst = grouped[:].rearrange("p a m t -> p (a m t)").bitcast(F32)
+            dst = dst.rearrange("p (a m u) -> p a m u", a=2, u=2)
+            src = bank[:].rearrange("p a u m -> p a m u")
+            if on_scalar:
+                nc.scalar.copy(out=dst, in_=src)
+            else:
+                nc.vector.tensor_copy(out=dst, in_=src)
+            quantize(codes, scales, col0, 256, grouped[:].rearrange("p a m t -> p (a m t)"))
+
+        def beliefs_group(g):
+            for h in range(2):
+                for j in range(JS):
+                    turn(braw[g, h], j, bq[j], bs[j], g * KP + h * 256, j < 2)
+
+        def unit(g, nb):
+            n0 = nb * NU
+            acc = psum.tile([P, 4, NU], F32, name="acc", bufs=5)
+            for t in range(4):
+                for j in range(JS):
+                    m0 = g * KP + t * P
+                    nc.tensor.matmul_mx(
+                        out=acc[:, t, :],
+                        lhsT=bq[j][:, m0 : m0 + P].bitcast(X4),
+                        lhsT_scale=bs[j][:, m0 : m0 + P],
+                        rhs=tq[j][:, n0 : n0 + NU].bitcast(X4),
+                        rhs_scale=ts[j][:, n0 : n0 + NU],
+                        start=(j == 0),
+                        stop=(j == JS - 1),
+                    )
+            c = n0 // 512
+            off = n0 - 512 * c
+            joint = stage.tile([P, NU, 4], BF16, name="joint", bufs=4, align_bytes=64)
+            nc.vector.tensor_tensor(
+                out=joint[:],
+                in0=acc[:].rearrange("p t n -> p n t"),
+                in1=lk[g, c][:, :, off : off + NU].rearrange("p t n -> p n t"),
+                op=ALU.mult,
+            )
+            quantize(jq[g], js[g], n0, NU, joint[:].rearrange("p n t -> p (n t)"))
+
+        def mix_pair(q):
+            for g in range(GS):
+                turn(mraw[q], g, mq[g], ms[g], q * 256, True)
+
+        def pool_rows(i):
+            raw = stage.tile([P, S], F32, name="raw", bufs=4)
+            sums = stage.tile([P, 3], F32, name="sums", bufs=4)
+            for c in range(3):
+                acc = psum.tile([P, 512], F32, name="acc", bufs=5)
+                for g in range(GS):
+                    nc.tensor.matmul_mx(
+                        out=acc[:],
+                        lhsT=mq[g][:, i * P : (i + 1) * P].bitcast(X4),
+                        lhsT_scale=ms[g][:, i * P : (i + 1) * P],
+                        rhs=jq[g][:, c * 512 : (c + 1) * 512].bitcast(X4),
+                        rhs_scale=js[g][:, c * 512 : (c + 1) * 512],
+                        start=(g == 0),
+                        stop=(g == GS - 1),
+                    )
+                dst = raw[:, c * 512 : (c + 1) * 512]
+                nc.scalar.activation(out=dst, in_=acc[:], func=ACT.Copy, accum_out=sums[:, c : c + 1])
+            total = stage.tile([P, 1], F32, name="total", bufs=4)
+            nc.vector.reduce_sum(out=total[:], in_=sums[:], axis=AX.X)
+            inverse = stage.tile([P, 1], F32, name="inverse", bufs=4)
+            nc.vector.reciprocal(out=inverse[:], in_=total[:])
+            res = stage.tile([P, S], F32, name="res", bufs=4)
+            nc.vector.tensor_scalar(
+                out=res[:], in0=raw[:], scalar1=inverse[:], scalar2=float(S), op0=ALU.mult, op1=ALU.mult
+            )
+            nc.sync.dma_start(out=o_view[i], in_=res[:])
+
+        trans_chunk(0)
+        beliefs_group(0)
+        beliefs_group(1)
+        for q in range(6):
+            if q + 1 < 6:
+                trans_chunk(q + 1)
+            for g in range(GS):
+                for nb in (2 * q, 2 * q + 1):
+                    unit(g, nb)
+        for q in range(4):
+            mix_pair(q)
+            pool_rows(2 * q)
+            pool_rows(2 * q + 1)

@@ -22,9 +22,10 @@ JS = S // KP
 GS = M // KP
 NU = 128
 CW = 256
+QS = S // CW
+UNITS = 4 * QS
 LOADS = ((0, 512), (512, 512), (1024, 512))
-WIDEN_ON_VECTOR = (10, 0, 2, 4, 0, 5)
-INTERLEAVE_ON_SCALAR = (1, 1, 2, 1, 2, 2)
+INTERLEAVE_ON_SCALAR = (1, 1, 1, 1, 1, 2)
 
 
 def tile_pooled_belief_update_s7_kernel(tc, beliefs, trans_bytes, trans_scale, like, mix, out):
@@ -34,6 +35,7 @@ def tile_pooled_belief_update_s7_kernel(tc, beliefs, trans_bytes, trans_scale, l
         stage = ctx.enter_context(tc.tile_pool(name="stage", bufs=4))
         psum = ctx.enter_context(tc.psum_pool(name="psum", bufs=1))
 
+        ctx.enter_context(tc.manual_schedule())
         ident = keep.tile([P, P], F32, name="ident")
         make_identity(nc, ident[:])
 
@@ -105,30 +107,39 @@ def tile_pooled_belief_update_s7_kernel(tc, beliefs, trans_bytes, trans_scale, l
                 out=codes[:, c0 : c0 + w].bitcast(X4), scales=scales[:, c0 : c0 + w], in_=src
             )
 
-        def trans_chunk(q):
-            c0, w = q * CW, CW
-            for j in range(JS):
-                c = c0 // 512
-                off = c0 - 512 * c
-                wide = stage.tile([P, 4, w], BF16, name="wide", bufs=6)
-                for t in range(4):
-                    src = tb[c, j][:, t, off : off + w].bitcast(F8)
-                    if 4 * j + t < WIDEN_ON_VECTOR[q]:
-                        nc.vector.tensor_scalar(
-                            out=wide[:, t, :], in0=src, scalar1=tscale[:, j, t : t + 1], scalar2=None, op0=ALU.mult
-                        )
-                    else:
-                        nc.scalar.activation(
-                            out=wide[:, t, :], in_=src, func=ACT.Copy, scale=tscale[:, j, t : t + 1]
-                        )
-                grouped = stage.tile([P, w, 4], BF16, name="tgroup", bufs=6, align_bytes=64)
-                if JS - j <= INTERLEAVE_ON_SCALAR[q]:
-                    nc.scalar.copy(out=grouped[:], in_=wide[:].rearrange("p t n -> p n t"))
-                else:
-                    nc.vector.tensor_copy(out=grouped[:], in_=wide[:].rearrange("p t n -> p n t"))
-                quantize(tq[j], ts[j], c0, w, grouped[:].rearrange("p n t -> p (n t)"))
+        wide = {}
+        tgroup = {}
 
-        def turn(raw, pass_index, codes, scales, col0, on_scalar):
+        def widen(q, j, first=0, last=4, on_vector=False):
+            if (q, j) not in wide:
+                w_tile = stage.tile([P, 4, CW], BF16, name="wide", bufs=9)
+                wide[q, j] = w_tile
+            c, off = divmod(q * CW, 512)
+            for t in range(first, last):
+                dst = wide[q, j][:, t, :]
+                src = tb[c, j][:, t, off : off + CW].bitcast(F8)
+                scale = tscale[:, j, t : t + 1]
+                if on_vector:
+                    nc.vector.tensor_scalar(out=dst, in0=src, scalar1=scale, scalar2=None, op0=ALU.mult)
+                else:
+                    nc.scalar.activation(out=dst, in_=src, func=ACT.Copy, scale=scale)
+
+        def interleave(q, j, on_scalar=False):
+            g_tile = stage.tile([P, CW, 4], BF16, name="tgroup", bufs=7, align_bytes=64)
+            tgroup[q, j] = g_tile
+            src = wide[q, j][:].rearrange("p t n -> p n t")
+            if on_scalar:
+                nc.scalar.copy(out=g_tile[:], in_=src)
+            else:
+                nc.vector.tensor_copy(out=g_tile[:], in_=src)
+
+        def quantize_trans(q, j):
+            quantize(tq[j], ts[j], q * CW, CW, tgroup[q, j][:].rearrange("p n t -> p (n t)"))
+
+        turned = {}
+        regrouped = {}
+
+        def turn(raw, pass_index):
             words = raw[:].rearrange("p a k -> p (a k)").bitcast(F32)
             row_words = raw.shape[2] // 2
             bank = psum.tile([P, 2, 2, P], F32, name="xt", bufs=3)
@@ -136,7 +147,10 @@ def tile_pooled_belief_update_s7_kernel(tc, beliefs, trans_bytes, trans_scale, l
                 for u in range(2):
                     w0 = a * row_words + 256 * pass_index
                     nc.tensor.transpose(bank[:, a, u, :], words[:, w0 + u : w0 + 256 : 2], ident[:])
-            grouped = stage.tile([P, 2, P, 4], BF16, name="bgroup", bufs=4, align_bytes=64)
+            return bank
+
+        def regroup(bank, on_scalar):
+            grouped = stage.tile([P, 2, P, 4], BF16, name="bgroup", bufs=6, align_bytes=64)
             dst = grouped[:].rearrange("p a m t -> p (a m t)").bitcast(F32)
             dst = dst.rearrange("p (a m u) -> p a m u", a=2, u=2)
             src = bank[:].rearrange("p a u m -> p a m u")
@@ -144,16 +158,40 @@ def tile_pooled_belief_update_s7_kernel(tc, beliefs, trans_bytes, trans_scale, l
                 nc.scalar.copy(out=dst, in_=src)
             else:
                 nc.vector.tensor_copy(out=dst, in_=src)
-            quantize(codes, scales, col0, 256, grouped[:].rearrange("p a m t -> p (a m t)"))
+            return grouped
 
-        def beliefs_group(g):
-            for h in range(2):
-                for j in range(JS):
-                    turn(braw[g, h], j, bq[j], bs[j], g * KP + h * 256, j < 2)
+        def turn_b(g, h, j):
+            turned["b", g, h, j] = turn(braw[g, h], j)
 
-        def unit(g, nb):
+        def regroup_b(g, h, j, on_scalar=True):
+            regrouped["b", g, h, j] = regroup(turned["b", g, h, j], on_scalar)
+
+        def quantize_b(g, h, j):
+            src = regrouped["b", g, h, j][:].rearrange("p a m t -> p (a m t)")
+            quantize(bq[j], bs[j], g * KP + h * 256, 256, src)
+
+        def turn_m(q, g):
+            turned["m", q, g] = turn(mraw[q], g)
+
+        def regroup_m(q, g, on_scalar=True):
+            regrouped["m", q, g] = regroup(turned["m", q, g], on_scalar)
+
+        def quantize_m(q, g):
+            src = regrouped["m", q, g][:].rearrange("p a m t -> p (a m t)")
+            quantize(mq[g], ms[g], q * 256, 256, src)
+
+        accs = {}
+        joints = {}
+
+        def place(u):
+            q, i = divmod(u, 4)
+            return i // 2, 2 * q + i % 2
+
+        def predict(u):
+            g, nb = place(u)
             n0 = nb * NU
             acc = psum.tile([P, 4, NU], F32, name="acc", bufs=5)
+            accs[u] = acc
             for t in range(4):
                 for j in range(JS):
                     m0 = g * KP + t * P
@@ -166,58 +204,160 @@ def tile_pooled_belief_update_s7_kernel(tc, beliefs, trans_bytes, trans_scale, l
                         start=(j == 0),
                         stop=(j == JS - 1),
                     )
-            c = n0 // 512
-            off = n0 - 512 * c
+
+        def multiply(u):
+            g, nb = place(u)
+            c, off = divmod(nb * NU, 512)
             joint = stage.tile([P, NU, 4], BF16, name="joint", bufs=4, align_bytes=64)
+            joints[u] = joint
             nc.vector.tensor_tensor(
                 out=joint[:],
-                in0=acc[:].rearrange("p t n -> p n t"),
+                in0=accs[u][:].rearrange("p t n -> p n t"),
                 in1=lk[g, c][:, :, off : off + NU].rearrange("p t n -> p n t"),
                 op=ALU.mult,
             )
-            quantize(jq[g], js[g], n0, NU, joint[:].rearrange("p n t -> p (n t)"))
 
-        def mix_pair(q):
+        def quantize_joint(u):
+            g, nb = place(u)
+            quantize(jq[g], js[g], nb * NU, NU, joints[u][:].rearrange("p n t -> p (n t)"))
+
+        raws = {}
+        sumss = {}
+        pools = {}
+        inverses = {}
+
+        def pool(i, c):
+            acc = psum.tile([P, 512], F32, name="acc", bufs=5)
+            pools[i, c] = acc
             for g in range(GS):
-                turn(mraw[q], g, mq[g], ms[g], q * 256, True)
+                nc.tensor.matmul_mx(
+                    out=acc[:],
+                    lhsT=mq[g][:, i * P : (i + 1) * P].bitcast(X4),
+                    lhsT_scale=ms[g][:, i * P : (i + 1) * P],
+                    rhs=jq[g][:, c * 512 : (c + 1) * 512].bitcast(X4),
+                    rhs_scale=js[g][:, c * 512 : (c + 1) * 512],
+                    start=(g == 0),
+                    stop=(g == GS - 1),
+                )
 
-        def pool_rows(i):
-            raw = stage.tile([P, S], F32, name="raw", bufs=4)
-            sums = stage.tile([P, 3], F32, name="sums", bufs=4)
-            for c in range(3):
-                acc = psum.tile([P, 512], F32, name="acc", bufs=5)
-                for g in range(GS):
-                    nc.tensor.matmul_mx(
-                        out=acc[:],
-                        lhsT=mq[g][:, i * P : (i + 1) * P].bitcast(X4),
-                        lhsT_scale=ms[g][:, i * P : (i + 1) * P],
-                        rhs=jq[g][:, c * 512 : (c + 1) * 512].bitcast(X4),
-                        rhs_scale=js[g][:, c * 512 : (c + 1) * 512],
-                        start=(g == 0),
-                        stop=(g == GS - 1),
-                    )
-                dst = raw[:, c * 512 : (c + 1) * 512]
-                nc.scalar.activation(out=dst, in_=acc[:], func=ACT.Copy, accum_out=sums[:, c : c + 1])
+        def drain(i, c):
+            if i not in raws:
+                raw = stage.tile([P, S], F32, name="raw", bufs=3)
+                sums = stage.tile([P, 3], F32, name="sums", bufs=4)
+                raws[i], sumss[i] = raw, sums
+            dst = raws[i][:, c * 512 : (c + 1) * 512]
+            nc.scalar.activation(out=dst, in_=pools[i, c][:], func=ACT.Copy, accum_out=sumss[i][:, c : c + 1])
+
+        def invert(i):
             total = stage.tile([P, 1], F32, name="total", bufs=4)
-            nc.vector.reduce_sum(out=total[:], in_=sums[:], axis=AX.X)
+            nc.vector.reduce_sum(out=total[:], in_=sumss[i][:], axis=AX.X)
             inverse = stage.tile([P, 1], F32, name="inverse", bufs=4)
             nc.vector.reciprocal(out=inverse[:], in_=total[:])
-            res = stage.tile([P, S], F32, name="res", bufs=4)
-            nc.vector.tensor_scalar(
-                out=res[:], in0=raw[:], scalar1=inverse[:], scalar2=float(S), op0=ALU.mult, op1=ALU.mult
-            )
-            nc.sync.dma_start(out=o_view[i], in_=res[:])
+            inverses[i] = inverse
 
-        trans_chunk(0)
-        beliefs_group(0)
-        beliefs_group(1)
-        for q in range(6):
-            if q + 1 < 6:
-                trans_chunk(q + 1)
-            for g in range(GS):
-                for nb in (2 * q, 2 * q + 1):
-                    unit(g, nb)
-        for q in range(4):
-            mix_pair(q)
-            pool_rows(2 * q)
-            pool_rows(2 * q + 1)
+        def normalise(i, pieces):
+            res = stage.tile([P, S], F32, name="res", bufs=4)
+            w = S // pieces
+            for k in range(pieces):
+                cols = slice(k * w, (k + 1) * w)
+                nc.vector.tensor_scalar(
+                    out=res[:, cols],
+                    in0=raws[i][:, cols],
+                    scalar1=inverses[i][:],
+                    scalar2=float(S),
+                    op0=ALU.mult,
+                    op1=ALU.mult,
+                )
+                nc.sync.dma_start(out=o_view[i][:, cols], in_=res[:, cols])
+
+        for t in (0, 2):
+            widen(0, t // 2, on_vector=True) if t == 0 else widen(0, 1, 0, 2, on_vector=True)
+        widen(1, 0)
+        interleave(0, 0)
+        widen(0, 1, 2, 4, on_vector=True)
+        widen(1, 1, 0, 2)
+        widen(0, 2)
+        quantize_trans(0, 0)
+        interleave(0, 1)
+        interleave(0, 2, on_scalar=True)
+        interleave(1, 0)
+        quantize_trans(0, 1)
+        quantize_trans(1, 0)
+        quantize_trans(0, 2)
+        for g in range(GS):
+            for h in range(2):
+                if (g, h) != (1, 1):
+                    for j in range(JS):
+                        turn_b(g, h, j)
+                        regroup_b(g, h, j, on_scalar=j < 2)
+                    if (g, h) == (0, 0):
+                        widen(1, 1, 2, 4)
+                        for j in range(JS):
+                            quantize_b(g, h, j)
+                        interleave(1, 1)
+                    elif (g, h) == (0, 1):
+                        widen(1, 2)
+                        quantize_b(g, h, 0)
+                        quantize_b(g, h, 1)
+                        quantize_trans(1, 1)
+                        quantize_b(g, h, 2)
+                    else:
+                        interleave(1, 2, on_scalar=True)
+                        quantize_b(g, h, 0)
+                        quantize_b(g, h, 1)
+                        quantize_b(g, h, 2)
+        turn_b(1, 1, 0)
+        turn_b(1, 1, 1)
+        regroup_b(1, 1, 0)
+        regroup_b(1, 1, 1)
+        turn_b(1, 1, 2)
+        regroup_b(1, 1, 2, False)
+        quantize_b(1, 1, 0)
+        quantize_b(1, 1, 1)
+        quantize_trans(1, 2)
+        quantize_b(1, 1, 2)
+        for j in range(JS):
+            widen(2, j)
+        interleave(2, 2, on_scalar=True)
+        for q in range(QS):
+            for i in range(4):
+                predict(4 * q + i)
+            if q == 2:
+                turn_m(0, 0)
+                turn_m(0, 1)
+                turn_m(1, 0)
+            if q == 4:
+                for k in range(3, 8):
+                    turn_m(k // 2, k % 2)
+                    regroup_m(k // 2, k % 2)
+            if 1 <= q and q + 1 < QS:
+                for j in range(JS):
+                    if JS - j > INTERLEAVE_ON_SCALAR[q + 1]:
+                        interleave(q + 1, j)
+                for j in range(JS):
+                    quantize_trans(q + 1, j)
+            if q + 3 < QS:
+                for j in range(JS):
+                    widen(q + 3, j)
+                for j in range(JS):
+                    if JS - j <= INTERLEAVE_ON_SCALAR[q + 3]:
+                        interleave(q + 3, j, on_scalar=True)
+            if q == 2:
+                for k in range(3):
+                    regroup_m(k // 2, k % 2)
+            for i in (0, 2):
+                multiply(4 * q + i)
+                multiply(4 * q + i + 1)
+                if q == 5:
+                    quantize_m(i // 2, 0)
+                    quantize_m(i // 2, 1)
+                quantize_joint(4 * q + i)
+                quantize_joint(4 * q + i + 1)
+        for k in range(4, 8):
+            quantize_m(k // 2, k % 2)
+        for i in range(R // P):
+            for c in range(3):
+                pool(i, c)
+                drain(i, c)
+            invert(i)
+            normalise(i, 3 if i == R // P - 1 else 1)

@@ -14,18 +14,26 @@ F8 = mybir.dt.float8_e4m3fn
 X4 = mybir.dt.float8_e4m3fn_x4
 ALU = mybir.AluOpType
 ACT = mybir.ActivationFunctionType
-AX = mybir.AxisListType
+AXIS = mybir.AxisListType
 
 P = 128
-KP = 512
-JS = S // KP
-GS = M // KP
-NU = 128
-CW = 256
-QS = S // CW
-UNITS = 4 * QS
-LOADS = ((0, 512), (512, 512), (1024, 512))
-INTERLEAVE_ON_SCALAR = (1, 1, 1, 1, 1, 2)
+T = 4
+PASS = P * T
+STATE_PASSES = S // PASS
+GROUPS = M // PASS
+BANK = 512
+CHUNK = 256
+CHUNKS = S // CHUNK
+UNIT = 128
+RUN = 4
+ROW_TILES = R // P
+
+TURN_BANKS = 3
+MIX_TURNS = {2: (0, 1, 2), 4: (3, 4, 5), 5: (6, 7)}
+
+
+def interleaved_by_scalar(chunk):
+    return (1, 2) if chunk == CHUNKS - 1 else (2,)
 
 
 def tile_pooled_belief_update_s7_kernel(tc, beliefs, trans_bytes, trans_scale, like, mix, out):
@@ -34,330 +42,296 @@ def tile_pooled_belief_update_s7_kernel(tc, beliefs, trans_bytes, trans_scale, l
         keep = ctx.enter_context(tc.tile_pool(name="keep", bufs=1))
         stage = ctx.enter_context(tc.tile_pool(name="stage", bufs=4))
         psum = ctx.enter_context(tc.psum_pool(name="psum", bufs=1))
-
         ctx.enter_context(tc.manual_schedule())
-        ident = keep.tile([P, P], F32, name="ident")
-        make_identity(nc, ident[:])
 
-        t_view = trans_bytes.rearrange("(j p t) n -> j p t n", p=P, t=4)
-        b_view = beliefs.rearrange("(g p t) k -> g p t k", p=P, t=4)
-        l_view = like.rearrange("(g p t) n -> g p t n", p=P, t=4)
-        m_view = mix.rearrange("(p i) m -> p i m", i=8)
-        o_view = out.rearrange("(p i) n -> i p n", i=8)
+        identity = keep.tile([P, P], F32, name="identity")
+        make_identity(nc, identity[:])
 
-        tscale = keep.tile([P, JS, 4], F32, name="tscale")
-        nc.sync.dma_start(out=tscale[:], in_=trans_scale.rearrange("(j p t) o -> p j (t o)", p=P, t=4))
+        trans_rows = trans_bytes.rearrange("(j p t) n -> j p t n", p=P, t=T)
+        belief_rows = beliefs.rearrange("(g p t) k -> g p t k", p=P, t=T)
+        like_rows = like.rearrange("(g p t) n -> g p t n", p=P, t=T)
+        mix_rows = mix.rearrange("(p i) m -> p i m", i=ROW_TILES)
+        out_rows = out.rearrange("(p i) n -> i p n", i=ROW_TILES)
 
-        tb = {}
-        lk = {}
-        braw = {}
-        mraw = {}
+        scale = keep.tile([P, STATE_PASSES, T], F32, name="scale")
+        nc.scalar.dma_start(out=scale[:], in_=trans_scale.rearrange("(j p t) o -> p j (t o)", p=P, t=T))
 
-        def load_t(c):
-            c0, w = LOADS[c]
-            for j in range(JS):
-                tile = keep.tile([P, 4, w], U8, name=f"tb_{c}_{j}")
-                nc.sync.dma_start(out=tile[:], in_=t_view[j][:, :, c0 : c0 + w])
-                tb[c, j] = tile
+        raw_bytes = {}
+        likelihood = {}
+        turn_rows = {}
 
-        def load_b(g):
-            for h in range(2):
-                tile = keep.tile([P, 2, S], BF16, name=f"braw_{g}_{h}")
-                nc.sync.dma_start(out=tile[:], in_=b_view[g][:, 2 * h : 2 * h + 2, :])
-                braw[g, h] = tile
+        def load_trans(part):
+            cols = slice(part * BANK, (part + 1) * BANK)
+            for j in range(STATE_PASSES):
+                tile = keep.tile([P, T, BANK], U8, name=f"bytes_{part}_{j}")
+                nc.sync.dma_start(out=tile[:], in_=trans_rows[j][:, :, cols])
+                raw_bytes[part, j] = tile
 
-        def load_l(g, c):
-            c0, w = LOADS[c]
-            tile = keep.tile([P, 4, w], BF16, name=f"lk_{g}_{c}")
-            nc.sync.dma_start(out=tile[:], in_=l_view[g][:, :, c0 : c0 + w])
-            lk[g, c] = tile
+        def load_beliefs(g):
+            for half in range(2):
+                tile = keep.tile([P, 2, S], BF16, name=f"beliefs_{g}_{half}")
+                nc.sync.dma_start(out=tile[:], in_=belief_rows[g][:, 2 * half : 2 * half + 2, :])
+                turn_rows["beliefs", 2 * g + half] = tile
 
-        def load_m(q):
-            tile = keep.tile([P, 2, M], BF16, name=f"mraw_{q}")
-            nc.sync.dma_start(out=tile[:], in_=m_view[:, 2 * q : 2 * q + 2, :])
-            mraw[q] = tile
+        def load_like(g, part):
+            cols = slice(part * BANK, (part + 1) * BANK)
+            tile = keep.tile([P, T, BANK], BF16, name=f"like_{g}_{part}")
+            nc.sync.dma_start(out=tile[:], in_=like_rows[g][:, :, cols])
+            likelihood[g, part] = tile
 
-        load_t(0)
-        load_b(0)
-        load_b(1)
-        load_l(0, 0)
-        load_t(1)
-        load_l(1, 0)
-        load_t(2)
-        load_l(0, 1)
-        load_l(1, 1)
-        load_m(0)
-        load_l(0, 2)
-        load_l(1, 2)
-        load_m(1)
-        load_m(2)
-        load_m(3)
+        def load_mix(pair):
+            tile = keep.tile([P, 2, M], BF16, name=f"mix_{pair}")
+            nc.sync.dma_start(out=tile[:], in_=mix_rows[:, 2 * pair : 2 * pair + 2, :])
+            turn_rows["mix", pair] = tile
 
-        tq = [keep.tile([P, S], U32, name=f"tq_{j}", align_bytes=64) for j in range(JS)]
-        ts = [keep.tile([P, S], U8, name=f"ts_{j}", align_bytes=64) for j in range(JS)]
-        bq = [keep.tile([P, M], U32, name=f"bq_{j}", align_bytes=64) for j in range(JS)]
-        bs = [keep.tile([P, M], U8, name=f"bs_{j}", align_bytes=64) for j in range(JS)]
-        mq = [keep.tile([P, R], U32, name=f"mq_{g}", align_bytes=64) for g in range(GS)]
-        ms = [keep.tile([P, R], U8, name=f"ms_{g}", align_bytes=64) for g in range(GS)]
-        jq = [keep.tile([P, S], U32, name=f"jq_{g}", align_bytes=64) for g in range(GS)]
-        js = [keep.tile([P, S], U8, name=f"js_{g}", align_bytes=64) for g in range(GS)]
+        load_trans(0)
+        load_beliefs(0)
+        load_beliefs(1)
+        load_like(0, 0)
+        load_trans(1)
+        load_like(1, 0)
+        load_trans(2)
+        load_like(0, 1)
+        load_like(1, 1)
+        load_mix(0)
+        load_mix(1)
+        load_like(0, 2)
+        load_like(1, 2)
+        load_mix(2)
+        load_mix(3)
 
-        def quantize(codes, scales, c0, w, src):
-            nc.vector.quantize_mx(
-                out=codes[:, c0 : c0 + w].bitcast(X4), scales=scales[:, c0 : c0 + w], in_=src
-            )
+        def operand(name, passes, width):
+            return [
+                (
+                    keep.tile([P, width], U32, name=f"{name}_codes_{k}", align_bytes=64),
+                    keep.tile([P, width], U8, name=f"{name}_scales_{k}", align_bytes=64),
+                )
+                for k in range(passes)
+            ]
 
-        wide = {}
-        tgroup = {}
+        trans_q = operand("trans", STATE_PASSES, S)
+        beliefs_q = operand("beliefs", STATE_PASSES, M)
+        mix_q = operand("mix", GROUPS, R)
+        joint_q = operand("joint", GROUPS, S)
 
-        def widen(q, j, first=0, last=4, on_vector=False):
-            if (q, j) not in wide:
-                w_tile = stage.tile([P, 4, CW], BF16, name="wide", bufs=9)
-                wide[q, j] = w_tile
-            c, off = divmod(q * CW, 512)
-            for t in range(first, last):
-                dst = wide[q, j][:, t, :]
-                src = tb[c, j][:, t, off : off + CW].bitcast(F8)
-                scale = tscale[:, j, t : t + 1]
+        def quantize(target, first, width, source):
+            codes, scales = target
+            cols = slice(first, first + width)
+            nc.vector.quantize_mx(out=codes[:, cols].bitcast(X4), scales=scales[:, cols], in_=source)
+
+        def multiply_mx(acc, stationary, moving, stationary_cols, moving_cols):
+            passes = len(stationary)
+            for k in range(passes):
+                nc.tensor.matmul_mx(
+                    out=acc,
+                    lhsT=stationary[k][0][:, stationary_cols].bitcast(X4),
+                    lhsT_scale=stationary[k][1][:, stationary_cols],
+                    rhs=moving[k][0][:, moving_cols].bitcast(X4),
+                    rhs_scale=moving[k][1][:, moving_cols],
+                    start=(k == 0),
+                    stop=(k == passes - 1),
+                )
+
+        widened = {}
+        interleaved = {}
+
+        def widen(chunk, j, slots=range(T), on_vector=False):
+            if (chunk, j) not in widened:
+                widened[chunk, j] = stage.tile([P, T, CHUNK], BF16, name="wide", bufs=9)
+            part, first = divmod(chunk * CHUNK, BANK)
+            for t in slots:
+                target = widened[chunk, j][:, t, :]
+                source = raw_bytes[part, j][:, t, first : first + CHUNK].bitcast(F8)
+                factor = scale[:, j, t : t + 1]
                 if on_vector:
-                    nc.vector.tensor_scalar(out=dst, in0=src, scalar1=scale, scalar2=None, op0=ALU.mult)
+                    nc.vector.tensor_scalar(out=target, in0=source, scalar1=factor, scalar2=None, op0=ALU.mult)
                 else:
-                    nc.scalar.activation(out=dst, in_=src, func=ACT.Copy, scale=scale)
+                    nc.scalar.activation(out=target, in_=source, func=ACT.Copy, scale=factor)
 
-        def interleave(q, j, on_scalar=False):
-            g_tile = stage.tile([P, CW, 4], BF16, name="tgroup", bufs=7, align_bytes=64)
-            tgroup[q, j] = g_tile
-            src = wide[q, j][:].rearrange("p t n -> p n t")
-            if on_scalar:
-                nc.scalar.copy(out=g_tile[:], in_=src)
+        def interleave(chunk, j):
+            tile = stage.tile([P, CHUNK, T], BF16, name="interleaved", bufs=7, align_bytes=64)
+            interleaved[chunk, j] = tile
+            target = tile[:].rearrange("p (c i) t -> p c t i", i=RUN)
+            source = widened[chunk, j][:].rearrange("p t (c i) -> p c t i", i=RUN)
+            if j in interleaved_by_scalar(chunk):
+                nc.scalar.copy(out=target, in_=source)
             else:
-                nc.vector.tensor_copy(out=g_tile[:], in_=src)
+                nc.vector.tensor_copy(out=target, in_=source)
 
-        def quantize_trans(q, j):
-            quantize(tq[j], ts[j], q * CW, CW, tgroup[q, j][:].rearrange("p n t -> p (n t)"))
+        def quantize_trans(chunk, j):
+            quantize(trans_q[j], chunk * CHUNK, CHUNK, interleaved[chunk, j][:].rearrange("p n t -> p (n t)"))
 
         turned = {}
         regrouped = {}
 
-        def turn(raw, pass_index):
-            words = raw[:].rearrange("p a k -> p (a k)").bitcast(F32)
-            row_words = raw.shape[2] // 2
-            bank = psum.tile([P, 2, 2, P], F32, name="xt", bufs=3)
+        def turn(name, pair, k):
+            rows = turn_rows[name, pair]
+            words = rows[:].rearrange("p a k -> p (a k)").bitcast(F32)
+            row_words = rows.shape[2] // 2
+            bank = psum.tile([P, 2, 2, P], F32, name="turned", bufs=TURN_BANKS)
+            turned[name, pair, k] = bank
             for a in range(2):
                 for u in range(2):
-                    w0 = a * row_words + 256 * pass_index
-                    nc.tensor.transpose(bank[:, a, u, :], words[:, w0 + u : w0 + 256 : 2], ident[:])
-            return bank
+                    first = a * row_words + 2 * P * k
+                    nc.tensor.transpose(bank[:, a, u, :], words[:, first + u : first + 2 * P : 2], identity[:])
 
-        def regroup(bank, on_scalar):
-            grouped = stage.tile([P, 2, P, 4], BF16, name="bgroup", bufs=6, align_bytes=64)
-            dst = grouped[:].rearrange("p a m t -> p (a m t)").bitcast(F32)
-            dst = dst.rearrange("p (a m u) -> p a m u", a=2, u=2)
-            src = bank[:].rearrange("p a u m -> p a m u")
-            if on_scalar:
-                nc.scalar.copy(out=dst, in_=src)
+        def regroup(name, pair, k, on_vector=False):
+            tile = stage.tile([P, 2 * P, T], BF16, name="regrouped", bufs=6, align_bytes=64)
+            regrouped[name, pair, k] = tile
+            target = tile[:].rearrange("p c t -> p (c t)").bitcast(F32)
+            target = target.rearrange("p (a c u) -> p a c u", a=2, u=2)
+            source = turned[name, pair, k][:].rearrange("p a u c -> p a c u")
+            if on_vector:
+                nc.vector.tensor_copy(out=target, in_=source)
             else:
-                nc.vector.tensor_copy(out=dst, in_=src)
-            return grouped
+                nc.scalar.copy(out=target, in_=source)
 
-        def turn_b(g, h, j):
-            turned["b", g, h, j] = turn(braw[g, h], j)
+        def quantize_turned(name, pair, k):
+            target = beliefs_q[k] if name == "beliefs" else mix_q[k]
+            quantize(target, pair * 2 * P, 2 * P, regrouped[name, pair, k][:].rearrange("p c t -> p (c t)"))
 
-        def regroup_b(g, h, j, on_scalar=True):
-            regrouped["b", g, h, j] = regroup(turned["b", g, h, j], on_scalar)
+        predicted = {}
+        joint = {}
 
-        def quantize_b(g, h, j):
-            src = regrouped["b", g, h, j][:].rearrange("p a m t -> p (a m t)")
-            quantize(bq[j], bs[j], g * KP + h * 256, 256, src)
+        def place(unit):
+            chunk, i = divmod(unit, 4)
+            return i // 2, 2 * chunk + i % 2
 
-        def turn_m(q, g):
-            turned["m", q, g] = turn(mraw[q], g)
+        def predict(unit):
+            g, n = place(unit)
+            acc = psum.tile([P, T, UNIT], F32, name="acc", bufs=5)
+            predicted[unit] = acc
+            for t in range(T):
+                first = g * PASS + t * P
+                multiply_mx(
+                    acc[:, t, :], beliefs_q, trans_q, slice(first, first + P), slice(n * UNIT, (n + 1) * UNIT)
+                )
 
-        def regroup_m(q, g, on_scalar=True):
-            regrouped["m", q, g] = regroup(turned["m", q, g], on_scalar)
-
-        def quantize_m(q, g):
-            src = regrouped["m", q, g][:].rearrange("p a m t -> p (a m t)")
-            quantize(mq[g], ms[g], q * 256, 256, src)
-
-        accs = {}
-        joints = {}
-
-        def place(u):
-            q, i = divmod(u, 4)
-            return i // 2, 2 * q + i % 2
-
-        def predict(u):
-            g, nb = place(u)
-            n0 = nb * NU
-            acc = psum.tile([P, 4, NU], F32, name="acc", bufs=5)
-            accs[u] = acc
-            for t in range(4):
-                for j in range(JS):
-                    m0 = g * KP + t * P
-                    nc.tensor.matmul_mx(
-                        out=acc[:, t, :],
-                        lhsT=bq[j][:, m0 : m0 + P].bitcast(X4),
-                        lhsT_scale=bs[j][:, m0 : m0 + P],
-                        rhs=tq[j][:, n0 : n0 + NU].bitcast(X4),
-                        rhs_scale=ts[j][:, n0 : n0 + NU],
-                        start=(j == 0),
-                        stop=(j == JS - 1),
-                    )
-
-        def multiply(u):
-            g, nb = place(u)
-            c, off = divmod(nb * NU, 512)
-            joint = stage.tile([P, NU, 4], BF16, name="joint", bufs=4, align_bytes=64)
-            joints[u] = joint
+        def times_like(unit):
+            g, n = place(unit)
+            part, first = divmod(n * UNIT, BANK)
+            tile = stage.tile([P, UNIT, T], BF16, name="joint", bufs=4, align_bytes=64)
+            joint[unit] = tile
             nc.vector.tensor_tensor(
-                out=joint[:],
-                in0=accs[u][:].rearrange("p t n -> p n t"),
-                in1=lk[g, c][:, :, off : off + NU].rearrange("p t n -> p n t"),
+                out=tile[:].rearrange("p (c i) t -> p c t i", i=RUN),
+                in0=predicted[unit][:].rearrange("p t (c i) -> p c t i", i=RUN),
+                in1=likelihood[g, part][:, :, first : first + UNIT].rearrange("p t (c i) -> p c t i", i=RUN),
                 op=ALU.mult,
             )
 
-        def quantize_joint(u):
-            g, nb = place(u)
-            quantize(jq[g], js[g], nb * NU, NU, joints[u][:].rearrange("p n t -> p (n t)"))
+        def quantize_joint(unit):
+            g, n = place(unit)
+            quantize(joint_q[g], n * UNIT, UNIT, joint[unit][:].rearrange("p n t -> p (n t)"))
 
-        raws = {}
-        sumss = {}
-        pools = {}
-        inverses = {}
-
-        def pool(i, c):
-            acc = psum.tile([P, 512], F32, name="acc", bufs=5)
-            pools[i, c] = acc
-            for g in range(GS):
-                nc.tensor.matmul_mx(
-                    out=acc[:],
-                    lhsT=mq[g][:, i * P : (i + 1) * P].bitcast(X4),
-                    lhsT_scale=ms[g][:, i * P : (i + 1) * P],
-                    rhs=jq[g][:, c * 512 : (c + 1) * 512].bitcast(X4),
-                    rhs_scale=js[g][:, c * 512 : (c + 1) * 512],
-                    start=(g == 0),
-                    stop=(g == GS - 1),
-                )
-
-        def drain(i, c):
-            if i not in raws:
-                raw = stage.tile([P, S], F32, name="raw", bufs=3)
-                sums = stage.tile([P, 3], F32, name="sums", bufs=4)
-                raws[i], sumss[i] = raw, sums
-            dst = raws[i][:, c * 512 : (c + 1) * 512]
-            nc.scalar.activation(out=dst, in_=pools[i, c][:], func=ACT.Copy, accum_out=sumss[i][:, c : c + 1])
-
-        def invert(i):
+        def pool_rows(i, pieces):
+            pooled = stage.tile([P, S], F32, name="pooled", bufs=3)
+            sums = stage.tile([P, S // BANK], F32, name="sums", bufs=4)
+            for c in range(S // BANK):
+                cols = slice(c * BANK, (c + 1) * BANK)
+                acc = psum.tile([P, BANK], F32, name="acc", bufs=5)
+                multiply_mx(acc[:], mix_q, joint_q, slice(i * P, (i + 1) * P), cols)
+                nc.scalar.activation(out=pooled[:, cols], in_=acc[:], func=ACT.Copy, accum_out=sums[:, c : c + 1])
             total = stage.tile([P, 1], F32, name="total", bufs=4)
-            nc.vector.reduce_sum(out=total[:], in_=sumss[i][:], axis=AX.X)
+            nc.vector.reduce_sum(out=total[:], in_=sums[:], axis=AXIS.X)
             inverse = stage.tile([P, 1], F32, name="inverse", bufs=4)
             nc.vector.reciprocal(out=inverse[:], in_=total[:])
-            inverses[i] = inverse
-
-        def normalise(i, pieces):
-            res = stage.tile([P, S], F32, name="res", bufs=4)
-            w = S // pieces
+            result = stage.tile([P, S], F32, name="result", bufs=4)
+            width = S // pieces
             for k in range(pieces):
-                cols = slice(k * w, (k + 1) * w)
+                cols = slice(k * width, (k + 1) * width)
                 nc.vector.tensor_scalar(
-                    out=res[:, cols],
-                    in0=raws[i][:, cols],
-                    scalar1=inverses[i][:],
+                    out=result[:, cols],
+                    in0=pooled[:, cols],
+                    scalar1=inverse[:],
                     scalar2=float(S),
                     op0=ALU.mult,
                     op1=ALU.mult,
                 )
-                nc.sync.dma_start(out=o_view[i][:, cols], in_=res[:, cols])
+                nc.sync.dma_start(out=out_rows[i][:, cols], in_=result[:, cols])
 
-        for t in (0, 2):
-            widen(0, t // 2, on_vector=True) if t == 0 else widen(0, 1, 0, 2, on_vector=True)
+        widen(0, 0, on_vector=True)
+        widen(0, 1, range(2), on_vector=True)
         widen(1, 0)
         interleave(0, 0)
-        widen(0, 1, 2, 4, on_vector=True)
-        widen(1, 1, 0, 2)
+        widen(0, 1, range(2, T), on_vector=True)
+        widen(1, 1, range(2))
         widen(0, 2)
         quantize_trans(0, 0)
         interleave(0, 1)
-        interleave(0, 2, on_scalar=True)
+        interleave(0, 2)
         interleave(1, 0)
         quantize_trans(0, 1)
         quantize_trans(1, 0)
         quantize_trans(0, 2)
-        for g in range(GS):
-            for h in range(2):
-                if (g, h) != (1, 1):
-                    for j in range(JS):
-                        turn_b(g, h, j)
-                        regroup_b(g, h, j, on_scalar=j < 2)
-                    if (g, h) == (0, 0):
-                        widen(1, 1, 2, 4)
-                        for j in range(JS):
-                            quantize_b(g, h, j)
-                        interleave(1, 1)
-                    elif (g, h) == (0, 1):
-                        widen(1, 2)
-                        quantize_b(g, h, 0)
-                        quantize_b(g, h, 1)
-                        quantize_trans(1, 1)
-                        quantize_b(g, h, 2)
-                    else:
-                        interleave(1, 2, on_scalar=True)
-                        quantize_b(g, h, 0)
-                        quantize_b(g, h, 1)
-                        quantize_b(g, h, 2)
-        turn_b(1, 1, 0)
-        turn_b(1, 1, 1)
-        regroup_b(1, 1, 0)
-        regroup_b(1, 1, 1)
-        turn_b(1, 1, 2)
-        regroup_b(1, 1, 2, False)
-        quantize_b(1, 1, 0)
-        quantize_b(1, 1, 1)
-        quantize_trans(1, 2)
-        quantize_b(1, 1, 2)
-        for j in range(JS):
+
+        for pair in range(4):
+            for j in range(STATE_PASSES):
+                turn("beliefs", pair, j)
+                regroup("beliefs", pair, j, on_vector=j == 2)
+            if pair == 0:
+                widen(1, 1, range(2, T))
+            elif pair == 1:
+                widen(1, 2)
+            elif pair == 2:
+                interleave(1, 2)
+            quantize_turned("beliefs", pair, 0)
+            quantize_turned("beliefs", pair, 1)
+            if pair == 1:
+                quantize_trans(1, 1)
+            elif pair == 3:
+                quantize_trans(1, 2)
+            quantize_turned("beliefs", pair, 2)
+            if pair == 0:
+                interleave(1, 1)
+
+        for j in range(STATE_PASSES):
             widen(2, j)
-        interleave(2, 2, on_scalar=True)
-        for q in range(QS):
-            for i in range(4):
-                predict(4 * q + i)
-            if q == 2:
-                turn_m(0, 0)
-                turn_m(0, 1)
-                turn_m(1, 0)
-            if q == 4:
-                for k in range(3, 8):
-                    turn_m(k // 2, k % 2)
-                    regroup_m(k // 2, k % 2)
-            if 1 <= q and q + 1 < QS:
-                for j in range(JS):
-                    if JS - j > INTERLEAVE_ON_SCALAR[q + 1]:
-                        interleave(q + 1, j)
-                for j in range(JS):
-                    quantize_trans(q + 1, j)
-            if q + 3 < QS:
-                for j in range(JS):
-                    widen(q + 3, j)
-                for j in range(JS):
-                    if JS - j <= INTERLEAVE_ON_SCALAR[q + 3]:
-                        interleave(q + 3, j, on_scalar=True)
-            if q == 2:
-                for k in range(3):
-                    regroup_m(k // 2, k % 2)
-            for i in (0, 2):
-                multiply(4 * q + i)
-                multiply(4 * q + i + 1)
-                if q == 5:
-                    quantize_m(i // 2, 0)
-                    quantize_m(i // 2, 1)
-                quantize_joint(4 * q + i)
-                quantize_joint(4 * q + i + 1)
-        for k in range(4, 8):
-            quantize_m(k // 2, k % 2)
-        for i in range(R // P):
-            for c in range(3):
-                pool(i, c)
-                drain(i, c)
-            invert(i)
-            normalise(i, 3 if i == R // P - 1 else 1)
+        interleave(2, 2)
+
+        for chunk in range(CHUNKS):
+            for unit in range(4 * chunk, 4 * chunk + 4):
+                predict(unit)
+            mix_banks = [divmod(bank, GROUPS) for bank in MIX_TURNS.get(chunk, ())]
+            for pair, g in mix_banks:
+                turn("mix", pair, g)
+
+            following = chunk + 1
+            woven = following == CHUNKS - 1
+            if 1 < following < CHUNKS:
+                for j in range(STATE_PASSES):
+                    if j not in interleaved_by_scalar(following):
+                        interleave(following, j)
+                if not woven:
+                    for j in range(STATE_PASSES):
+                        quantize_trans(following, j)
+
+            ahead = chunk + 3
+            if ahead < CHUNKS:
+                for j in range(STATE_PASSES):
+                    widen(ahead, j)
+            for pair, g in mix_banks:
+                regroup("mix", pair, g)
+            if ahead < CHUNKS:
+                for j in interleaved_by_scalar(ahead):
+                    interleave(ahead, j)
+
+            for half in range(2):
+                first = 4 * chunk + 2 * half
+                times_like(first)
+                times_like(first + 1)
+                if woven and half == 0:
+                    quantize_trans(following, 0)
+                if chunk == CHUNKS - 1:
+                    for bank in (0, 1) if half == 0 else (2,):
+                        quantize_turned("mix", *divmod(bank, GROUPS))
+                quantize_joint(first)
+                quantize_joint(first + 1)
+                if woven and half == 0:
+                    quantize_trans(following, 1)
+                    quantize_trans(following, 2)
+
+        for bank in range(3, ROW_TILES // 2 * GROUPS):
+            quantize_turned("mix", *divmod(bank, GROUPS))
+
+        for i in range(ROW_TILES):
+            pool_rows(i, pieces={0: 2, ROW_TILES - 1: 3}.get(i, 1))

from contextlib import ExitStack

import concourse.mybir as mybir
from concourse.masks import make_identity

M, S, R = 1024, 1536, 1024
FLOPS = 2 * M * S * S + 2 * R * M * S + 3 * M * S

F32 = mybir.dt.float32
BF16 = mybir.dt.bfloat16
U32 = mybir.dt.uint32
U8 = mybir.dt.uint8
F8 = mybir.dt.float8_e4m3fn
X4 = mybir.dt.float8_e4m3fn_x4
ALU = mybir.AluOpType
ACT = mybir.ActivationFunctionType
AXIS = mybir.AxisListType

P = 128
T = 4
PASS = P * T
STATE_PASSES = S // PASS
GROUPS = M // PASS
BANK = 512
CHUNK = 256
CHUNKS = S // CHUNK
UNIT = 128
RUN = 4
ROW_TILES = R // P

TURN_BANKS = 3
MIX_TURNS = {2: (0, 1, 2), 4: (3, 4, 5), 5: (6, 7)}


def interleaved_by_scalar(chunk):
    return (1, 2) if chunk == CHUNKS - 1 else (2,)


def tile_pooled_belief_update_s7_kernel(tc, beliefs, trans_bytes, trans_scale, like, mix, out):
    nc = tc.nc
    with ExitStack() as ctx:
        keep = ctx.enter_context(tc.tile_pool(name="keep", bufs=1))
        stage = ctx.enter_context(tc.tile_pool(name="stage", bufs=4))
        psum = ctx.enter_context(tc.psum_pool(name="psum", bufs=1))
        ctx.enter_context(tc.manual_schedule())

        identity = keep.tile([P, P], F32, name="identity")
        make_identity(nc, identity[:])

        trans_rows = trans_bytes.rearrange("(j p t) n -> j p t n", p=P, t=T)
        belief_rows = beliefs.rearrange("(g p t) k -> g p t k", p=P, t=T)
        like_rows = like.rearrange("(g p t) n -> g p t n", p=P, t=T)
        mix_rows = mix.rearrange("(p i) m -> p i m", i=ROW_TILES)
        out_rows = out.rearrange("(p i) n -> i p n", i=ROW_TILES)

        scale = keep.tile([P, STATE_PASSES, T], F32, name="scale")
        nc.scalar.dma_start(out=scale[:], in_=trans_scale.rearrange("(j p t) o -> p j (t o)", p=P, t=T))

        raw_bytes = {}
        likelihood = {}
        turn_rows = {}

        def load_trans(part):
            cols = slice(part * BANK, (part + 1) * BANK)
            for j in range(STATE_PASSES):
                tile = keep.tile([P, T, BANK], U8, name=f"bytes_{part}_{j}")
                nc.sync.dma_start(out=tile[:], in_=trans_rows[j][:, :, cols])
                raw_bytes[part, j] = tile

        def load_beliefs(g):
            for half in range(2):
                tile = keep.tile([P, 2, S], BF16, name=f"beliefs_{g}_{half}")
                nc.sync.dma_start(out=tile[:], in_=belief_rows[g][:, 2 * half : 2 * half + 2, :])
                turn_rows["beliefs", 2 * g + half] = tile

        def load_like(g, part):
            cols = slice(part * BANK, (part + 1) * BANK)
            tile = keep.tile([P, T, BANK], BF16, name=f"like_{g}_{part}")
            nc.sync.dma_start(out=tile[:], in_=like_rows[g][:, :, cols])
            likelihood[g, part] = tile

        def load_mix(pair):
            tile = keep.tile([P, 2, M], BF16, name=f"mix_{pair}")
            nc.sync.dma_start(out=tile[:], in_=mix_rows[:, 2 * pair : 2 * pair + 2, :])
            turn_rows["mix", pair] = tile

        load_trans(0)
        load_beliefs(0)
        load_beliefs(1)
        load_like(0, 0)
        load_trans(1)
        load_like(1, 0)
        load_trans(2)
        load_like(0, 1)
        load_like(1, 1)
        load_mix(0)
        load_mix(1)
        load_like(0, 2)
        load_like(1, 2)
        load_mix(2)
        load_mix(3)

        def operand(name, passes, width):
            return [
                (
                    keep.tile([P, width], U32, name=f"{name}_codes_{k}", align_bytes=64),
                    keep.tile([P, width], U8, name=f"{name}_scales_{k}", align_bytes=64),
                )
                for k in range(passes)
            ]

        trans_q = operand("trans", STATE_PASSES, S)
        beliefs_q = operand("beliefs", STATE_PASSES, M)
        mix_q = operand("mix", GROUPS, R)
        joint_q = operand("joint", GROUPS, S)

        def quantize(target, first, width, source):
            codes, scales = target
            cols = slice(first, first + width)
            nc.vector.quantize_mx(out=codes[:, cols].bitcast(X4), scales=scales[:, cols], in_=source)

        def multiply_mx(acc, stationary, moving, stationary_cols, moving_cols):
            passes = len(stationary)
            for k in range(passes):
                nc.tensor.matmul_mx(
                    out=acc,
                    lhsT=stationary[k][0][:, stationary_cols].bitcast(X4),
                    lhsT_scale=stationary[k][1][:, stationary_cols],
                    rhs=moving[k][0][:, moving_cols].bitcast(X4),
                    rhs_scale=moving[k][1][:, moving_cols],
                    start=(k == 0),
                    stop=(k == passes - 1),
                )

        widened = {}
        interleaved = {}

        def widen(chunk, j, slots=range(T), on_vector=False):
            if (chunk, j) not in widened:
                widened[chunk, j] = stage.tile([P, T, CHUNK], BF16, name="wide", bufs=9)
            part, first = divmod(chunk * CHUNK, BANK)
            for t in slots:
                target = widened[chunk, j][:, t, :]
                source = raw_bytes[part, j][:, t, first : first + CHUNK].bitcast(F8)
                factor = scale[:, j, t : t + 1]
                if on_vector:
                    nc.vector.tensor_scalar(out=target, in0=source, scalar1=factor, scalar2=None, op0=ALU.mult)
                else:
                    nc.scalar.activation(out=target, in_=source, func=ACT.Copy, scale=factor)

        def interleave(chunk, j):
            tile = stage.tile([P, CHUNK, T], BF16, name="interleaved", bufs=7, align_bytes=64)
            interleaved[chunk, j] = tile
            target = tile[:].rearrange("p (c i) t -> p c t i", i=RUN)
            source = widened[chunk, j][:].rearrange("p t (c i) -> p c t i", i=RUN)
            if j in interleaved_by_scalar(chunk):
                nc.scalar.copy(out=target, in_=source)
            else:
                nc.vector.tensor_copy(out=target, in_=source)

        def quantize_trans(chunk, j):
            quantize(trans_q[j], chunk * CHUNK, CHUNK, interleaved[chunk, j][:].rearrange("p n t -> p (n t)"))

        turned = {}
        regrouped = {}

        def turn(name, pair, k):
            rows = turn_rows[name, pair]
            words = rows[:].rearrange("p a k -> p (a k)").bitcast(F32)
            row_words = rows.shape[2] // 2
            bank = psum.tile([P, 2, 2, P], F32, name="turned", bufs=TURN_BANKS)
            turned[name, pair, k] = bank
            for a in range(2):
                for u in range(2):
                    first = a * row_words + 2 * P * k
                    nc.tensor.transpose(bank[:, a, u, :], words[:, first + u : first + 2 * P : 2], identity[:])

        def regroup(name, pair, k, on_vector=False):
            tile = stage.tile([P, 2 * P, T], BF16, name="regrouped", bufs=6, align_bytes=64)
            regrouped[name, pair, k] = tile
            target = tile[:].rearrange("p c t -> p (c t)").bitcast(F32)
            target = target.rearrange("p (a c u) -> p a c u", a=2, u=2)
            source = turned[name, pair, k][:].rearrange("p a u c -> p a c u")
            if on_vector:
                nc.vector.tensor_copy(out=target, in_=source)
            else:
                nc.scalar.copy(out=target, in_=source)

        def quantize_turned(name, pair, k):
            target = beliefs_q[k] if name == "beliefs" else mix_q[k]
            quantize(target, pair * 2 * P, 2 * P, regrouped[name, pair, k][:].rearrange("p c t -> p (c t)"))

        predicted = {}
        joint = {}

        def place(unit):
            chunk, i = divmod(unit, 4)
            return i // 2, 2 * chunk + i % 2

        def predict(unit):
            g, n = place(unit)
            acc = psum.tile([P, T, UNIT], F32, name="acc", bufs=5)
            predicted[unit] = acc
            for t in range(T):
                first = g * PASS + t * P
                multiply_mx(
                    acc[:, t, :], beliefs_q, trans_q, slice(first, first + P), slice(n * UNIT, (n + 1) * UNIT)
                )

        def times_like(unit):
            g, n = place(unit)
            part, first = divmod(n * UNIT, BANK)
            tile = stage.tile([P, UNIT, T], BF16, name="joint", bufs=4, align_bytes=64)
            joint[unit] = tile
            nc.vector.tensor_tensor(
                out=tile[:].rearrange("p (c i) t -> p c t i", i=RUN),
                in0=predicted[unit][:].rearrange("p t (c i) -> p c t i", i=RUN),
                in1=likelihood[g, part][:, :, first : first + UNIT].rearrange("p t (c i) -> p c t i", i=RUN),
                op=ALU.mult,
            )

        def quantize_joint(unit):
            g, n = place(unit)
            quantize(joint_q[g], n * UNIT, UNIT, joint[unit][:].rearrange("p n t -> p (n t)"))

        def pool_rows(i, pieces):
            pooled = stage.tile([P, S], F32, name="pooled", bufs=3)
            sums = stage.tile([P, S // BANK], F32, name="sums", bufs=4)
            for c in range(S // BANK):
                cols = slice(c * BANK, (c + 1) * BANK)
                acc = psum.tile([P, BANK], F32, name="acc", bufs=5)
                multiply_mx(acc[:], mix_q, joint_q, slice(i * P, (i + 1) * P), cols)
                nc.scalar.activation(out=pooled[:, cols], in_=acc[:], func=ACT.Copy, accum_out=sums[:, c : c + 1])
            total = stage.tile([P, 1], F32, name="total", bufs=4)
            nc.vector.reduce_sum(out=total[:], in_=sums[:], axis=AXIS.X)
            inverse = stage.tile([P, 1], F32, name="inverse", bufs=4)
            nc.vector.reciprocal(out=inverse[:], in_=total[:])
            result = stage.tile([P, S], F32, name="result", bufs=4)
            width = S // pieces
            for k in range(pieces):
                cols = slice(k * width, (k + 1) * width)
                nc.vector.tensor_scalar(
                    out=result[:, cols],
                    in0=pooled[:, cols],
                    scalar1=inverse[:],
                    scalar2=float(S),
                    op0=ALU.mult,
                    op1=ALU.mult,
                )
                nc.sync.dma_start(out=out_rows[i][:, cols], in_=result[:, cols])

        widen(0, 0, on_vector=True)
        widen(0, 1, range(2), on_vector=True)
        widen(1, 0)
        interleave(0, 0)
        widen(0, 1, range(2, T), on_vector=True)
        widen(1, 1, range(2))
        widen(0, 2)
        quantize_trans(0, 0)
        interleave(0, 1)
        interleave(0, 2)
        interleave(1, 0)
        quantize_trans(0, 1)
        quantize_trans(1, 0)
        quantize_trans(0, 2)

        for pair in range(4):
            for j in range(STATE_PASSES):
                turn("beliefs", pair, j)
                regroup("beliefs", pair, j, on_vector=j == 2)
            if pair == 0:
                widen(1, 1, range(2, T))
            elif pair == 1:
                widen(1, 2)
            elif pair == 2:
                interleave(1, 2)
            quantize_turned("beliefs", pair, 0)
            quantize_turned("beliefs", pair, 1)
            if pair == 1:
                quantize_trans(1, 1)
            elif pair == 3:
                quantize_trans(1, 2)
            quantize_turned("beliefs", pair, 2)
            if pair == 0:
                interleave(1, 1)

        for j in range(STATE_PASSES):
            widen(2, j)
        interleave(2, 2)

        for chunk in range(CHUNKS):
            for unit in range(4 * chunk, 4 * chunk + 4):
                predict(unit)
            mix_banks = [divmod(bank, GROUPS) for bank in MIX_TURNS.get(chunk, ())]
            for pair, g in mix_banks:
                turn("mix", pair, g)

            following = chunk + 1
            woven = following == CHUNKS - 1
            if 1 < following < CHUNKS:
                for j in range(STATE_PASSES):
                    if j not in interleaved_by_scalar(following):
                        interleave(following, j)
                if not woven:
                    for j in range(STATE_PASSES):
                        quantize_trans(following, j)

            ahead = chunk + 3
            if ahead < CHUNKS:
                for j in range(STATE_PASSES):
                    widen(ahead, j)
            for pair, g in mix_banks:
                regroup("mix", pair, g)
            if ahead < CHUNKS:
                for j in interleaved_by_scalar(ahead):
                    interleave(ahead, j)

            for half in range(2):
                first = 4 * chunk + 2 * half
                times_like(first)
                times_like(first + 1)
                if woven and half == 0:
                    quantize_trans(following, 0)
                if chunk == CHUNKS - 1:
                    for bank in (0, 1) if half == 0 else (2,):
                        quantize_turned("mix", *divmod(bank, GROUPS))
                quantize_joint(first)
                quantize_joint(first + 1)
                if woven and half == 0:
                    quantize_trans(following, 1)
                    quantize_trans(following, 2)

        for bank in range(3, ROW_TILES // 2 * GROUPS):
            quantize_turned("mix", *divmod(bank, GROUPS))

        for i in range(ROW_TILES):
            pool_rows(i, pieces={0: 2, ROW_TILES - 1: 3}.get(i, 1))
